import numpy as np
import ml_dtypes


def mxq(x, axis, fmt="e4m3"):
    dtype, down = {"e4m3": (ml_dtypes.float8_e4m3fn, 7), "e5m2": (ml_dtypes.float8_e5m2, 14)}[fmt]
    v = np.moveaxis(np.asarray(x, np.float32).astype(ml_dtypes.bfloat16).astype(np.float64), axis, -1)
    blocks = v.reshape(v.shape[:-1] + (-1, 32))
    amax = np.abs(blocks).max(-1, keepdims=True)
    byte = np.maximum(np.where(amax > 0, np.frexp(amax)[1] - 1 + 127, 0) - down, 1)
    scale = np.exp2(byte - 127.0)
    codes = (blocks / scale).astype(np.float32).astype(dtype).astype(np.float64)
    return np.moveaxis((codes * scale).reshape(v.shape), -1, axis)


WIDE = False


def mx_kscale(k):
    if not WIDE:
        return np.ones(k)
    levels = np.array([10, -10, 5, -5, 0])
    if k % 512:
        return np.exp2(np.random.permutation(np.resize(levels, k // 32))).repeat(32)
    a = np.empty((k // 512, 16))
    for p in range(k // 512):
        a[p, :8] = np.random.permutation(np.resize(levels, 8))
        for g in range(8):
            far = levels[np.abs(levels - a[p, g]) >= 10]
            a[p, g + 8] = far[np.random.randint(len(far))]
    return np.exp2(a.ravel()).repeat(32)


def f64(x):
    return np.asarray(x).astype(np.float64)


def striped(idx):
    return np.tile(idx.reshape(-1, 16).T, (8, 1)).astype(np.uint16)


def unstriped(offs):
    return offs[:16].T.reshape(-1).astype(np.int64)


def pack_weight(w):
    k, n = w.shape
    w = f64(np.asarray(w, np.float32).astype(ml_dtypes.bfloat16)).reshape(k // 32, 32, n)
    amax = np.abs(w).max(1)
    byte = np.clip(np.where(amax > 0, np.frexp(amax)[1] - 1 + 127 - 7, 1), 1, 254)
    scaled = (w * np.exp2(127.0 - byte)[:, None, :]).reshape(k, n).astype(np.float32)
    words = np.ascontiguousarray(scaled.reshape(k // 512, 128, 4, n).transpose(0, 1, 3, 2)).astype(ml_dtypes.float8_e4m3fn).view(np.uint8)
    return words, np.ascontiguousarray(byte.astype(np.uint8).reshape(k // 512, 16, n))


def unpack_weight(words, scales):
    g, p, n, _ = words.shape
    vals = np.ascontiguousarray(words).view(ml_dtypes.float8_e4m3fn).astype(np.float64) * np.repeat(np.exp2(scales.astype(np.float64) - 127.0), 8, axis=1)[..., None]
    return vals.transpose(0, 1, 3, 2).reshape(g * 512, n)


H, K, T, S, N, D = 512, 512, 2048, 512, 256, 3
P = 2 ** 7


def setup_inputs():
    n = np.random.standard_normal
    s = mx_kscale(K)[:, None]
    u = mx_kscale(H)
    packed_xT = pack_weight(n((K, T)) * s)
    return {
        "x_words": packed_xT[0],
        "x_scales": packed_xT[1],
        "w1": (n((K, H)) / np.sqrt(K) / s).astype(np.float32),
        "wgt": (np.tile(np.random.uniform(0.1, 0.6, (D, 1, S)), (1, P, 1))).astype(np.float32),
        "unit": (np.random.uniform(0.5, 1.5, (H, 1)) * u[:, None]).astype(np.float32),
        "wo": (n((H, N)) / np.sqrt(H) / u[:, None]).astype(np.float32),
        "offs": striped(np.random.permutation(T)[:S]),
        "pos1": striped(np.random.permutation(S)[:S]),
        "pos2": striped(np.random.permutation(S)[:S]),
        "pos3": striped(np.random.permutation(S)[:S]),
    }


def reference(x_words, x_scales, w1, wgt, unit, wo, offs, pos1, pos2, pos3):
    xq = unpack_weight(x_words, x_scales)[:, unstriped(offs)]
    y = mxq(f64(w1), 0, "e4m3").T @ xq
    mean = y.mean(axis=1, keepdims=True)
    dev = y - mean
    dev2 = (dev) ** 2
    var = dev2.mean(axis=1, keepdims=True) + 0.05
    locg = (((dev - dev[:, unstriped(pos1)]) ** 2) * f64(wgt)[0, :1] + ((dev - dev[:, unstriped(pos2)]) ** 2) * f64(wgt)[1, :1] + ((dev - dev[:, unstriped(pos3)]) ** 2) * f64(wgt)[2, :1]) / var
    zz = f64(unit) * locg
    return mxq(f64(wo), 0, "e4m3").T @ mxq(zz, 0, "e4m3")

@@ -1,0 +1,223 @@
+from contextlib import ExitStack
+
+import concourse.mybir as mybir
+from concourse.masks import make_identity
+
+K, H, T, S, N, D = 512, 512, 2048, 512, 256, 3
+P = 128
+PACK = 4
+BLOCKS = S // P
+EPS = 0.05
+FLOPS = 2 * K * H * S + 2 * H * N * S
+
+F32 = mybir.dt.float32
+BF16 = mybir.dt.bfloat16
+I32 = mybir.dt.int32
+U32 = mybir.dt.uint32
+U16 = mybir.dt.uint16
+U8 = mybir.dt.uint8
+FP8X4 = mybir.dt.float8_e4m3fn_x4
+ALU = mybir.AluOpType
+ACT = mybir.ActivationFunctionType
+WINDOW = 2048
+
+
+def tile_picked_ymoran_geary_p_kernel(
+    tc, x_words, x_scales, w1, wgt, unit, wo, offs, pos1, pos2, pos3, out
+):
+    nc = tc.nc
+    with ExitStack() as ctx:
+        keep = ctx.enter_context(tc.tile_pool(name="keep", bufs=1))
+        psum = ctx.enter_context(tc.psum_pool(name="psum", bufs=1))
+
+        table_scales = keep.tile([P, T], U8, name="table_scales")
+        nc.vector.memset(table_scales[:].bitcast(I32), 0)
+        offs_sb = keep.tile([P, S // 16], U16, name="offs_sb")
+        nc.sync.dma_start(offs_sb[:], offs)
+        for q in range(4):
+            nc.scalar.dma_start(
+                table_scales[32 * q : 32 * q + 4, :].bitcast(I32),
+                x_scales[0, 4 * q : 4 * q + 4, :].bitcast(I32),
+            )
+        w1_raw = keep.tile([P, PACK, H], F32, name="w1_raw")
+        nc.sync.dma_start(w1_raw[:], w1.rearrange("(p j) c -> p j c", j=PACK))
+        table_words = keep.tile([P, T], I32, name="table_words")
+        nc.sync.dma_start(table_words[:], x_words[0].rearrange("p n t -> p (n t)").bitcast(I32))
+        lists = []
+        for d, pos in enumerate((pos1, pos2, pos3)):
+            pos_sb = keep.tile([P, S // 16], U16, name=f"pos_sb{d}")
+            nc.sync.dma_start(pos_sb[:], pos)
+            lists.append(pos_sb)
+        wo_raw = keep.tile([P, PACK, N], F32, name="wo_raw")
+        nc.sync.dma_start(wo_raw[:], wo.rearrange("(p j) m -> p j m", j=PACK))
+        unit_sb = keep.tile([P, PACK], F32, name="unit_sb")
+        nc.sync.dma_start(unit_sb[:], unit.rearrange("(p t) o -> p (t o)", t=PACK))
+        wgt_rows = keep.tile([P, P], F32, name="wgt_rows")
+        nc.vector.memset(wgt_rows[:], 0.0)
+        for d in range(D):
+            nc.sync.dma_start(
+                wgt_rows[BLOCKS * d : BLOCKS * (d + 1), :],
+                wgt[d, 0:1, :].rearrange("o (b j) -> (o b) j", j=P),
+            )
+        ident = keep.tile([P, P], F32, name="ident")
+        make_identity(nc, ident[:])
+
+        windows = []
+        for t in range(PACK):
+            win = keep.tile([P, WINDOW], F32, name=f"window{t}")
+            windows.append(win)
+
+        picked_scales = keep.tile([P, S], U8, name="picked_scales", align_bytes=64)
+        nc.vector.tensor_copy(picked_scales[:], table_scales[:].indirect(offs_sb[:]))
+
+        w1_bf = keep.tile([P, PACK, P, PACK], BF16, name="w1_bf", align_bytes=64)
+        w1_dst = w1_bf[:].rearrange("p t m j -> p m j t")
+        w1_src = w1_raw[:].rearrange("p j (m t) -> p m j t", t=PACK)
+        split = 80
+        nc.vector.tensor_copy(w1_dst[:, :split], w1_src[:, :split])
+        nc.scalar.copy(w1_dst[:, split:], w1_src[:, split:])
+        w1_codes = keep.tile([P, H], U32, name="w1_codes", align_bytes=64)
+        w1_scales = keep.tile([P, H], U8, name="w1_scales", align_bytes=64)
+        nc.vector.quantize_mx(
+            out=w1_codes[:].bitcast(FP8X4),
+            scales=w1_scales[:],
+            in_=w1_bf[:].rearrange("p t m j -> p (t m j)"),
+        )
+        picked_words = keep.tile([P, S], I32, name="picked_words", align_bytes=64)
+        nc.vector.tensor_copy(
+            picked_words[:].bitcast(U32), table_words[:].bitcast(U32).indirect(offs_sb[:])
+        )
+
+        sums = keep.tile([P, PACK], F32, name="sums")
+        for t in range(PACK):
+            y_bank = psum.tile([P, S], F32, name=f"y_bank{t}", tag=f"sum{t}")
+            cols = slice(t * P, (t + 1) * P)
+            nc.tensor.matmul_mx(
+                out=y_bank[:],
+                lhsT=w1_codes[:, cols].bitcast(FP8X4),
+                lhsT_scale=w1_scales[:, cols],
+                rhs=picked_words[:].bitcast(FP8X4),
+                rhs_scale=picked_scales[:],
+                start=True,
+                stop=True,
+            )
+            nc.scalar.activation(
+                out=windows[t][:, :S], in_=y_bank[:], func=ACT.Copy, accum_out=sums[:, t : t + 1]
+            )
+
+        wgt_bank = psum.tile([P, S], F32, name="wgt_bank", tag="diff0")
+        nc.tensor.transpose(wgt_bank[:, :P], wgt_rows[:], ident[:])
+        wgt_cols = keep.tile([P, D * BLOCKS], F32, name="wgt_cols")
+        nc.scalar.copy(wgt_cols[:], wgt_bank[:, : D * BLOCKS])
+
+        neg_mean = keep.tile([P, PACK], F32, name="neg_mean")
+        nc.scalar.activation(out=neg_mean[:], in_=sums[:], func=ACT.Copy, scale=-1.0 / S)
+        squares = keep.tile([P, PACK], F32, name="squares")
+        dev2 = keep.tile([P, S], F32, name="dev2")
+        for t in range(PACK):
+            nc.scalar.activation(
+                out=dev2[:],
+                in_=windows[t][:, :S],
+                func=ACT.Square,
+                bias=neg_mean[:, t : t + 1],
+                accum_out=squares[:, t : t + 1],
+            )
+        var = keep.tile([P, PACK], F32, name="var")
+        nc.scalar.activation(out=var[:], in_=squares[:], func=ACT.Copy, scale=1.0 / S, bias=EPS)
+        inv_var = keep.tile([P, PACK], F32, name="inv_var")
+        nc.vector.reciprocal(inv_var[:], var[:])
+        factor = keep.tile([P, PACK], F32, name="factor")
+        nc.vector.tensor_tensor(factor[:], inv_var[:], unit_sb[:], ALU.mult)
+
+        wo_bf = keep.tile([P, N, PACK], BF16, name="wo_bf", align_bytes=64)
+        nc.scalar.copy(
+            wo_bf[:].rearrange("p (c i) j -> p c j i", i=4),
+            wo_raw[:].rearrange("p j (c i) -> p c j i", i=4),
+        )
+        wo_codes = keep.tile([P, N], U32, name="wo_codes", align_bytes=64)
+        wo_scales = keep.tile([P, N], U8, name="wo_scales", align_bytes=64)
+        nc.vector.quantize_mx(
+            out=wo_codes[:].bitcast(FP8X4),
+            scales=wo_scales[:],
+            in_=wo_bf[:].rearrange("p m j -> p (m j)"),
+        )
+
+        sum_banks = [psum.tile([P, S], F32, name=f"sum_bank{b}", tag=f"sum{b}") for b in range(BLOCKS)]
+        for d in range(D):
+            diff_banks = [
+                psum.tile([P, S], F32, name=f"diff_bank{d}_{b}", tag=f"diff{b}") for b in range(BLOCKS)
+            ]
+            for b in range(BLOCKS):
+                for t in range(PACK):
+                    nc.tensor.matmul(
+                        diff_banks[b][:, t * P : (t + 1) * P],
+                        windows[t][:, b * P : (b + 1) * P],
+                        ident[:],
+                        is_transpose=True,
+                        start=(t == 0),
+                        stop=False,
+                    )
+            for t in range(PACK):
+                negated = keep.tile([P, S], F32, name=f"negated{d}_{t}")
+                nc.vector.tensor_scalar(
+                    negated[:], windows[t][:].indirect(lists[d][:]), -1.0, 0.0, ALU.mult, ALU.add
+                )
+                for b in range(BLOCKS):
+                    nc.tensor.matmul(
+                        diff_banks[b][:, t * P : (t + 1) * P],
+                        negated[:, b * P : (b + 1) * P],
+                        ident[:],
+                        is_transpose=True,
+                        start=False,
+                        stop=(t == PACK - 1),
+                    )
+            for b in range(BLOCKS):
+                squared = keep.tile([P, S], F32, name=f"squared{d}_{b}")
+                nc.scalar.activation(out=squared[:], in_=diff_banks[b][:], func=ACT.Square)
+                weighted = keep.tile([P, S], F32, name=f"weighted{d}_{b}")
+                w_col = wgt_cols[:, BLOCKS * d + b : BLOCKS * d + b + 1]
+                if d == 0:
+                    nc.scalar.activation(out=weighted[:], in_=squared[:], func=ACT.Copy, scale=w_col)
+                else:
+                    nc.vector.tensor_scalar(weighted[:], squared[:], w_col, None, ALU.mult)
+                for t in range(PACK):
+                    nc.tensor.matmul(
+                        sum_banks[b][:, t * P : (t + 1) * P],
+                        weighted[:, t * P : (t + 1) * P],
+                        ident[:],
+                        is_transpose=True,
+                        start=(d == 0 and t == 0),
+                        stop=(d == D - 1 and t == PACK - 1),
+                    )
+
+        out_view = out.rearrange("(h p) j -> p h j", p=P)
+        for b in range(BLOCKS):
+            zz = keep.tile([P, P, PACK], BF16, name=f"zz{b}", align_bytes=64)
+            nc.vector.tensor_tensor(
+                zz[:],
+                sum_banks[b][:].rearrange("p (t j) -> p j t", t=PACK),
+                factor[:].unsqueeze(1).to_broadcast([P, P, PACK]),
+                ALU.mult,
+            )
+            zz_codes = keep.tile([P, P], U32, name=f"zz_codes{b}", align_bytes=64)
+            zz_scales = keep.tile([P, P], U8, name=f"zz_scales{b}", align_bytes=64)
+            nc.vector.quantize_mx(
+                out=zz_codes[:].bitcast(FP8X4),
+                scales=zz_scales[:],
+                in_=zz[:].rearrange("p j t -> p (j t)"),
+            )
+            out_bank = psum.tile([P, S], F32, name=f"out_bank{b}", tag=f"diff{b}")
+            for h in range(N // P):
+                cols = slice(h * P, (h + 1) * P)
+                nc.tensor.matmul_mx(
+                    out=out_bank[:, cols],
+                    lhsT=wo_codes[:, cols].bitcast(FP8X4),
+                    lhsT_scale=wo_scales[:, cols],
+                    rhs=zz_codes[:].bitcast(FP8X4),
+                    rhs_scale=zz_scales[:],
+                    start=True,
+                    stop=True,
+                )
+            result = keep.tile([P, N // P, P], F32, name=f"result{b}")
+            nc.scalar.copy(result[:].rearrange("p h j -> p (h j)"), out_bank[:, :N])
+            nc.sync.dma_start(out_view[:, :, b * P : (b + 1) * P], result[:])

@@ -30,35 +30,26 @@ def tile_picked_ymoran_geary_p_kernel(
         keep = ctx.enter_context(tc.tile_pool(name="keep", bufs=1))
         psum = ctx.enter_context(tc.psum_pool(name="psum", bufs=1))
 
-        table_scales = keep.tile([P, T], U8, name="table_scales")
-        nc.vector.memset(table_scales[:].bitcast(I32), 0)
+        table_scales = keep.tile([P, T], U8, name="table_scales", tag="scales_then_small")
+        nc.vector.memset(table_scales[:, : T // 2].bitcast(I32), 0)
+        nc.gpsimd.memset(table_scales[:, T // 2 :].bitcast(I32), 0)
         offs_sb = keep.tile([P, S // 16], U16, name="offs_sb")
         nc.sync.dma_start(offs_sb[:], offs)
+        lists = [keep.tile([P, S // 16], U16, name=f"pos_sb{d}") for d in range(D)]
+        nc.sync.dma_start(lists[0][:], pos1)
+        nc.sync.dma_start(lists[1][:], pos2)
+        w1_raw = keep.tile([P, PACK, H], F32, name="w1_raw")
+        nc.sync.dma_start(w1_raw[:], w1.rearrange("(p j) c -> p j c", j=PACK))
         for q in range(4):
-            nc.scalar.dma_start(
+            nc.sync.dma_start(
                 table_scales[32 * q : 32 * q + 4, :].bitcast(I32),
                 x_scales[0, 4 * q : 4 * q + 4, :].bitcast(I32),
             )
-        w1_raw = keep.tile([P, PACK, H], F32, name="w1_raw")
-        nc.sync.dma_start(w1_raw[:], w1.rearrange("(p j) c -> p j c", j=PACK))
         table_words = keep.tile([P, T], I32, name="table_words")
         nc.sync.dma_start(table_words[:], x_words[0].rearrange("p n t -> p (n t)").bitcast(I32))
-        lists = []
-        for d, pos in enumerate((pos1, pos2, pos3)):
-            pos_sb = keep.tile([P, S // 16], U16, name=f"pos_sb{d}")
-            nc.sync.dma_start(pos_sb[:], pos)
-            lists.append(pos_sb)
         wo_raw = keep.tile([P, PACK, N], F32, name="wo_raw")
         nc.sync.dma_start(wo_raw[:], wo.rearrange("(p j) m -> p j m", j=PACK))
-        unit_sb = keep.tile([P, PACK], F32, name="unit_sb")
-        nc.sync.dma_start(unit_sb[:], unit.rearrange("(p t) o -> p (t o)", t=PACK))
-        wgt_rows = keep.tile([P, P], F32, name="wgt_rows")
-        nc.vector.memset(wgt_rows[:], 0.0)
-        for d in range(D):
-            nc.sync.dma_start(
-                wgt_rows[BLOCKS * d : BLOCKS * (d + 1), :],
-                wgt[d, 0:1, :].rearrange("o (b j) -> (o b) j", j=P),
-            )
+        nc.sync.dma_start(lists[2][:], pos3)
         ident = keep.tile([P, P], F32, name="ident")
         make_identity(nc, ident[:])
 
@@ -69,6 +60,17 @@ def tile_picked_ymoran_geary_p_kernel(
 
         picked_scales = keep.tile([P, S], U8, name="picked_scales", align_bytes=64)
         nc.vector.tensor_copy(picked_scales[:], table_scales[:].indirect(offs_sb[:]))
+
+        small = keep.tile([P, P + PACK], F32, name="small", tag="scales_then_small")
+        nc.vector.memset(small[:], 0.0)
+        wgt_rows = small[:, :P]
+        unit_sb = small[:, P:]
+        row_step = P + 1
+        nc.sync.dma_start(
+            small[: D * BLOCKS, :P],
+            wgt.rearrange("d r (b j) -> (d r b) j", j=P)[0 : (D * BLOCKS - 1) * row_step + 1 : row_step, :],
+        )
+        nc.sync.dma_start(unit_sb, unit.rearrange("(p t) o -> p (t o)", t=PACK))
 
         w1_bf = keep.tile([P, PACK, P, PACK], BF16, name="w1_bf", align_bytes=64)
         w1_dst = w1_bf[:].rearrange("p t m j -> p m j t")
@@ -84,53 +86,15 @@ def tile_picked_ymoran_geary_p_kernel(
             in_=w1_bf[:].rearrange("p t m j -> p (t m j)"),
         )
         picked_words = keep.tile([P, S], I32, name="picked_words", align_bytes=64)
-        nc.vector.tensor_copy(
-            picked_words[:].bitcast(U32), table_words[:].bitcast(U32).indirect(offs_sb[:])
-        )
-
-        sums = keep.tile([P, PACK], F32, name="sums")
-        for t in range(PACK):
-            y_bank = psum.tile([P, S], F32, name=f"y_bank{t}", tag=f"sum{t}")
-            cols = slice(t * P, (t + 1) * P)
-            nc.tensor.matmul_mx(
-                out=y_bank[:],
-                lhsT=w1_codes[:, cols].bitcast(FP8X4),
-                lhsT_scale=w1_scales[:, cols],
-                rhs=picked_words[:].bitcast(FP8X4),
-                rhs_scale=picked_scales[:],
-                start=True,
-                stop=True,
+        half = S // 2
+        for u in range(2):
+            nc.vector.tensor_copy(
+                picked_words[:, u * half : (u + 1) * half].bitcast(U32),
+                table_words[:].bitcast(U32).indirect(offs_sb[:, u * half // 16 : (u + 1) * half // 16]),
             )
-            nc.scalar.activation(
-                out=windows[t][:, :S], in_=y_bank[:], func=ACT.Copy, accum_out=sums[:, t : t + 1]
-            )
-
-        wgt_bank = psum.tile([P, S], F32, name="wgt_bank", tag="diff0")
-        nc.tensor.transpose(wgt_bank[:, :P], wgt_rows[:], ident[:])
-        wgt_cols = keep.tile([P, D * BLOCKS], F32, name="wgt_cols")
-        nc.scalar.copy(wgt_cols[:], wgt_bank[:, : D * BLOCKS])
-
-        neg_mean = keep.tile([P, PACK], F32, name="neg_mean")
-        nc.scalar.activation(out=neg_mean[:], in_=sums[:], func=ACT.Copy, scale=-1.0 / S)
-        squares = keep.tile([P, PACK], F32, name="squares")
-        dev2 = keep.tile([P, S], F32, name="dev2")
-        for t in range(PACK):
-            nc.scalar.activation(
-                out=dev2[:],
-                in_=windows[t][:, :S],
-                func=ACT.Square,
-                bias=neg_mean[:, t : t + 1],
-                accum_out=squares[:, t : t + 1],
-            )
-        var = keep.tile([P, PACK], F32, name="var")
-        nc.scalar.activation(out=var[:], in_=squares[:], func=ACT.Copy, scale=1.0 / S, bias=EPS)
-        inv_var = keep.tile([P, PACK], F32, name="inv_var")
-        nc.vector.reciprocal(inv_var[:], var[:])
-        factor = keep.tile([P, PACK], F32, name="factor")
-        nc.vector.tensor_tensor(factor[:], inv_var[:], unit_sb[:], ALU.mult)
 
         wo_bf = keep.tile([P, N, PACK], BF16, name="wo_bf", align_bytes=64)
-        nc.scalar.copy(
+        nc.vector.tensor_copy(
             wo_bf[:].rearrange("p (c i) j -> p c j i", i=4),
             wo_raw[:].rearrange("p j (c i) -> p c j i", i=4),
         )
@@ -142,63 +106,153 @@ def tile_picked_ymoran_geary_p_kernel(
             in_=wo_bf[:].rearrange("p m j -> p (m j)"),
         )
 
-        sum_banks = [psum.tile([P, S], F32, name=f"sum_bank{b}", tag=f"sum{b}") for b in range(BLOCKS)]
-        for d in range(D):
-            diff_banks = [
-                psum.tile([P, S], F32, name=f"diff_bank{d}_{b}", tag=f"diff{b}") for b in range(BLOCKS)
-            ]
-            for b in range(BLOCKS):
-                for t in range(PACK):
-                    nc.tensor.matmul(
-                        diff_banks[b][:, t * P : (t + 1) * P],
-                        windows[t][:, b * P : (b + 1) * P],
-                        ident[:],
-                        is_transpose=True,
-                        start=(t == 0),
-                        stop=False,
-                    )
-            for t in range(PACK):
-                negated = keep.tile([P, S], F32, name=f"negated{d}_{t}")
-                nc.vector.tensor_scalar(
-                    negated[:], windows[t][:].indirect(lists[d][:]), -1.0, 0.0, ALU.mult, ALU.add
+        sums = keep.tile([P, PACK], F32, name="sums")
+        for t in range(PACK):
+            y_bank = psum.tile([P, S], F32, name=f"y_bank{t}", tag=f"sum{t}")
+            cols = slice(t * P, (t + 1) * P)
+            width = half if t == 0 else S
+            for j0 in range(0, S, width):
+                nc.tensor.matmul_mx(
+                    out=y_bank[:, j0 : j0 + width],
+                    lhsT=w1_codes[:, cols].bitcast(FP8X4),
+                    lhsT_scale=w1_scales[:, cols],
+                    rhs=picked_words[:, j0 : j0 + width].bitcast(FP8X4),
+                    rhs_scale=picked_scales[:, j0 : j0 + width],
+                    start=True,
+                    stop=True,
                 )
-                for b in range(BLOCKS):
-                    nc.tensor.matmul(
-                        diff_banks[b][:, t * P : (t + 1) * P],
-                        negated[:, b * P : (b + 1) * P],
-                        ident[:],
-                        is_transpose=True,
-                        start=False,
-                        stop=(t == PACK - 1),
-                    )
+            nc.scalar.activation(
+                out=windows[t][:, :S], in_=y_bank[:], func=ACT.Copy, accum_out=sums[:, t : t + 1]
+            )
+
+        wgt_bank = psum.tile([P, S], F32, name="wgt_bank", tag="spare")
+        nc.tensor.transpose(wgt_bank[:, :P], wgt_rows, ident[:])
+        wgt_cols = keep.tile([P, D * BLOCKS], F32, name="wgt_cols")
+        nc.scalar.copy(wgt_cols[:], wgt_bank[:, : D * BLOCKS])
+
+        neg_mean = keep.tile([P, PACK], F32, name="neg_mean")
+        nc.scalar.activation(out=neg_mean[:], in_=sums[:], func=ACT.Copy, scale=-1.0 / S)
+        squares = keep.tile([P, PACK], F32, name="squares")
+        dev2 = keep.tile([P, S], F32, name="dev2")
+
+        sum_banks = [psum.tile([P, S], F32, name=f"sum_bank{b}", tag=f"sum{b}") for b in range(BLOCKS)]
+        units = PACK * D
+        squared = {}
+        gathered = {}
+        weighted = {}
+
+        def differences(n):
+            t, d = divmod(n, D)
+            diff_bank = psum.tile([P, S], F32, name=f"diff_bank{n}", tag=f"diff{n % 3}")
             for b in range(BLOCKS):
-                squared = keep.tile([P, S], F32, name=f"squared{d}_{b}")
-                nc.scalar.activation(out=squared[:], in_=diff_banks[b][:], func=ACT.Square)
-                weighted = keep.tile([P, S], F32, name=f"weighted{d}_{b}")
+                nc.tensor.matmul(
+                    diff_bank[:, b * P : (b + 1) * P],
+                    windows[t][:, b * P : (b + 1) * P],
+                    ident[:],
+                    is_transpose=True,
+                    start=(b == 0),
+                    stop=False,
+                )
+            if n == 0:
+                gathered[0] = keep.tile([P, D + 1, S], F32, name="negated0")
+            elif d == 1 and t >= 1:
+                gathered[t] = keep.tile([P, D, S], F32, name=f"negated{t}", tag=f"squared{n - D}")
+            negated = gathered[0][:, n, :] if n <= D else gathered[(n - 1) // D][:, (n - 1) % D, :]
+            nc.vector.tensor_scalar(
+                negated, windows[t][:].indirect(lists[d][:]), -1.0, 0.0, ALU.mult, ALU.add
+            )
+            for b in range(BLOCKS):
+                nc.tensor.matmul(
+                    diff_bank[:, b * P : (b + 1) * P],
+                    negated[:, b * P : (b + 1) * P],
+                    ident[:],
+                    is_transpose=True,
+                    start=False,
+                    stop=(b == BLOCKS - 1),
+                )
+            squared[n] = keep.tile([P, S], F32, name=f"squared{n}", tag=f"squared{n}")
+            width = half if n == units - 1 else S
+            for j0 in range(0, S, width):
+                nc.scalar.activation(
+                    out=squared[n][:, j0 : j0 + width], in_=diff_bank[:, j0 : j0 + width], func=ACT.Square
+                )
+
+        def weigh_and_add(n):
+            t, d = divmod(n, D)
+            weighted[n] = keep.tile([P, S], F32, name=f"weighted{n}")
+            for b in range(BLOCKS):
+                cols = slice(b * P, (b + 1) * P)
                 w_col = wgt_cols[:, BLOCKS * d + b : BLOCKS * d + b + 1]
-                if d == 0:
-                    nc.scalar.activation(out=weighted[:], in_=squared[:], func=ACT.Copy, scale=w_col)
-                else:
-                    nc.vector.tensor_scalar(weighted[:], squared[:], w_col, None, ALU.mult)
-                for t in range(PACK):
-                    nc.tensor.matmul(
-                        sum_banks[b][:, t * P : (t + 1) * P],
-                        weighted[:, t * P : (t + 1) * P],
-                        ident[:],
-                        is_transpose=True,
-                        start=(d == 0 and t == 0),
-                        stop=(d == D - 1 and t == PACK - 1),
+                if d == 1:
+                    nc.vector.scalar_tensor_tensor(
+                        weighted[n][:, cols], squared[n][:, cols], w_col, weighted[n - 1][:, cols], ALU.mult, ALU.add
                     )
+                elif n == units - 1:
+                    nc.vector.tensor_scalar(weighted[n][:, cols], squared[n][:, cols], w_col, None, ALU.mult)
+                else:
+                    nc.scalar.activation(
+                        out=weighted[n][:, cols], in_=squared[n][:, cols], func=ACT.Copy, scale=w_col
+                    )
+            if d == 0:
+                return
+            for b in range(BLOCKS):
+                nc.tensor.matmul(
+                    sum_banks[b][:, t * P : (t + 1) * P],
+                    weighted[n][:, b * P : (b + 1) * P],
+                    ident[:],
+                    is_transpose=True,
+                    start=(n == 1),
+                    stop=(n == units - 1),
+                )
+
+        def sum_of_squares(t):
+            nc.scalar.activation(
+                out=dev2[:],
+                in_=windows[t][:, :S],
+                func=ACT.Square,
+                bias=neg_mean[:, t : t + 1],
+                accum_out=squares[:, t : t + 1],
+            )
+
+        for t in range(PACK):
+            n = D * t
+            differences(n)
+            if t == 0:
+                sum_of_squares(t)
+            else:
+                weigh_and_add(n - 1)
+            weigh_and_add(n)
+            differences(n + 1)
+            if t > 0:
+                sum_of_squares(t)
+            weigh_and_add(n + 1)
+            differences(n + 2)
+        weigh_and_add(units - 1)
+        var = keep.tile([P, PACK], F32, name="var")
+        nc.vector.tensor_scalar(var[:], squares[:], 1.0 / S, EPS, ALU.mult, ALU.add)
+        inv_var = keep.tile([P, PACK], F32, name="inv_var")
+        nc.vector.reciprocal(inv_var[:], var[:])
+        factor = keep.tile([P, PACK], F32, name="factor")
+        nc.vector.tensor_tensor(factor[:], inv_var[:], unit_sb, ALU.mult)
 
         out_view = out.rearrange("(h p) j -> p h j", p=P)
-        for b in range(BLOCKS):
-            zz = keep.tile([P, P, PACK], BF16, name=f"zz{b}", align_bytes=64)
-            nc.vector.tensor_tensor(
-                zz[:],
-                sum_banks[b][:].rearrange("p (t j) -> p j t", t=PACK),
-                factor[:].unsqueeze(1).to_broadcast([P, P, PACK]),
-                ALU.mult,
+        zz_tiles = [keep.tile([P, P, PACK], BF16, name=f"zz{b}", align_bytes=64) for b in range(BLOCKS)]
+        for t in range(PACK):
+            nc.scalar.activation(
+                out=zz_tiles[BLOCKS - 1][:, :, t],
+                in_=sum_banks[BLOCKS - 1][:, t * P : (t + 1) * P],
+                func=ACT.Copy,
+                scale=factor[:, t : t + 1],
             )
+        for b in range(BLOCKS):
+            zz = zz_tiles[b]
+            if b < BLOCKS - 1:
+                nc.vector.tensor_tensor(
+                    zz[:],
+                    sum_banks[b][:].rearrange("p (t j) -> p j t", t=PACK),
+                    factor[:].unsqueeze(1).to_broadcast([P, P, PACK]),
+                    ALU.mult,
+                )
             zz_codes = keep.tile([P, P], U32, name=f"zz_codes{b}", align_bytes=64)
             zz_scales = keep.tile([P, P], U8, name=f"zz_scales{b}", align_bytes=64)
             nc.vector.quantize_mx(
@@ -206,7 +260,7 @@ def tile_picked_ymoran_geary_p_kernel(
                 scales=zz_scales[:],
                 in_=zz[:].rearrange("p j t -> p (j t)"),
             )
-            out_bank = psum.tile([P, S], F32, name=f"out_bank{b}", tag=f"diff{b}")
+            out_bank = psum.tile([P, S], F32, name=f"out_bank{b}", tag=f"diff{b}" if b < 3 else "spare")
             for h in range(N // P):
                 cols = slice(h * P, (h + 1) * P)
                 nc.tensor.matmul_mx(

@@ -6,8 +6,15 @@ from concourse.masks import make_identity
 K, H, T, S, N, D = 512, 512, 2048, 512, 256, 3
 P = 128
 PACK = 4
+QUADRANT = 32
+STRIPE = 16
 BLOCKS = S // P
-EPS = 0.05
+HALF = S // 2
+STEPS = PACK * D
+VAR_FLOOR = 0.05
+WINDOW = 2048
+DIFF_BANKS = 3
+W1_VECTOR_SHARE = 80
 FLOPS = 2 * K * H * S + 2 * H * N * S
 
 F32 = mybir.dt.float32
@@ -19,7 +26,10 @@ U8 = mybir.dt.uint8
 FP8X4 = mybir.dt.float8_e4m3fn_x4
 ALU = mybir.AluOpType
 ACT = mybir.ActivationFunctionType
-WINDOW = 2048
+
+
+def span(index, width):
+    return slice(index * width, (index + 1) * width)
 
 
 def tile_picked_ymoran_geary_p_kernel(
@@ -30,20 +40,20 @@ def tile_picked_ymoran_geary_p_kernel(
         keep = ctx.enter_context(tc.tile_pool(name="keep", bufs=1))
         psum = ctx.enter_context(tc.psum_pool(name="psum", bufs=1))
 
-        table_scales = keep.tile([P, T], U8, name="table_scales", tag="scales_then_small")
+        table_scales = keep.tile([P, T], U8, name="table_scales", tag="scales_then_rows")
         nc.vector.memset(table_scales[:, : T // 2].bitcast(I32), 0)
         nc.gpsimd.memset(table_scales[:, T // 2 :].bitcast(I32), 0)
-        offs_sb = keep.tile([P, S // 16], U16, name="offs_sb")
+        offs_sb = keep.tile([P, S // STRIPE], U16, name="offs_sb")
         nc.sync.dma_start(offs_sb[:], offs)
-        lists = [keep.tile([P, S // 16], U16, name=f"pos_sb{d}") for d in range(D)]
+        lists = [keep.tile([P, S // STRIPE], U16, name=f"pos_sb{d}") for d in range(D)]
         nc.sync.dma_start(lists[0][:], pos1)
         nc.sync.dma_start(lists[1][:], pos2)
         w1_raw = keep.tile([P, PACK, H], F32, name="w1_raw")
         nc.sync.dma_start(w1_raw[:], w1.rearrange("(p j) c -> p j c", j=PACK))
-        for q in range(4):
+        for q in range(P // QUADRANT):
             nc.sync.dma_start(
-                table_scales[32 * q : 32 * q + 4, :].bitcast(I32),
-                x_scales[0, 4 * q : 4 * q + 4, :].bitcast(I32),
+                table_scales[QUADRANT * q : QUADRANT * q + 4, :].bitcast(I32),
+                x_scales[0, span(q, 4), :].bitcast(I32),
             )
         table_words = keep.tile([P, T], I32, name="table_words")
         nc.sync.dma_start(table_words[:], x_words[0].rearrange("p n t -> p (n t)").bitcast(I32))
@@ -53,31 +63,27 @@ def tile_picked_ymoran_geary_p_kernel(
         ident = keep.tile([P, P], F32, name="ident")
         make_identity(nc, ident[:])
 
-        windows = []
-        for t in range(PACK):
-            win = keep.tile([P, WINDOW], F32, name=f"window{t}")
-            windows.append(win)
+        windows = [keep.tile([P, WINDOW], F32, name=f"window{t}") for t in range(PACK)]
 
         picked_scales = keep.tile([P, S], U8, name="picked_scales", align_bytes=64)
         nc.vector.tensor_copy(picked_scales[:], table_scales[:].indirect(offs_sb[:]))
 
-        small = keep.tile([P, P + PACK], F32, name="small", tag="scales_then_small")
-        nc.vector.memset(small[:], 0.0)
-        wgt_rows = small[:, :P]
-        unit_sb = small[:, P:]
-        row_step = P + 1
+        rows = keep.tile([P, P + PACK], F32, name="rows", tag="scales_then_rows")
+        nc.vector.memset(rows[:], 0.0)
+        wgt_rows = rows[:, :P]
+        unit_sb = rows[:, P:]
+        piece_step = P + 1
         nc.sync.dma_start(
-            small[: D * BLOCKS, :P],
-            wgt.rearrange("d r (b j) -> (d r b) j", j=P)[0 : (D * BLOCKS - 1) * row_step + 1 : row_step, :],
+            rows[: D * BLOCKS, :P],
+            wgt.rearrange("d r (b j) -> (d r b) j", j=P)[0 : (D * BLOCKS - 1) * piece_step + 1 : piece_step, :],
         )
         nc.sync.dma_start(unit_sb, unit.rearrange("(p t) o -> p (t o)", t=PACK))
 
         w1_bf = keep.tile([P, PACK, P, PACK], BF16, name="w1_bf", align_bytes=64)
         w1_dst = w1_bf[:].rearrange("p t m j -> p m j t")
         w1_src = w1_raw[:].rearrange("p j (m t) -> p m j t", t=PACK)
-        split = 80
-        nc.vector.tensor_copy(w1_dst[:, :split], w1_src[:, :split])
-        nc.scalar.copy(w1_dst[:, split:], w1_src[:, split:])
+        nc.vector.tensor_copy(w1_dst[:, :W1_VECTOR_SHARE], w1_src[:, :W1_VECTOR_SHARE])
+        nc.scalar.copy(w1_dst[:, W1_VECTOR_SHARE:], w1_src[:, W1_VECTOR_SHARE:])
         w1_codes = keep.tile([P, H], U32, name="w1_codes", align_bytes=64)
         w1_scales = keep.tile([P, H], U8, name="w1_scales", align_bytes=64)
         nc.vector.quantize_mx(
@@ -85,12 +91,12 @@ def tile_picked_ymoran_geary_p_kernel(
             scales=w1_scales[:],
             in_=w1_bf[:].rearrange("p t m j -> p (t m j)"),
         )
+
         picked_words = keep.tile([P, S], I32, name="picked_words", align_bytes=64)
-        half = S // 2
-        for u in range(2):
+        for u in range(S // HALF):
             nc.vector.tensor_copy(
-                picked_words[:, u * half : (u + 1) * half].bitcast(U32),
-                table_words[:].bitcast(U32).indirect(offs_sb[:, u * half // 16 : (u + 1) * half // 16]),
+                picked_words[:, span(u, HALF)].bitcast(U32),
+                table_words[:].bitcast(U32).indirect(offs_sb[:, span(u, HALF // STRIPE)]),
             )
 
         wo_bf = keep.tile([P, N, PACK], BF16, name="wo_bf", align_bytes=64)
@@ -106,24 +112,34 @@ def tile_picked_ymoran_geary_p_kernel(
             in_=wo_bf[:].rearrange("p m j -> p (m j)"),
         )
 
-        sums = keep.tile([P, PACK], F32, name="sums")
+        row_sums = keep.tile([P, PACK + 2], F32, name="row_sums")
+        y_copies = {}
         for t in range(PACK):
-            y_bank = psum.tile([P, S], F32, name=f"y_bank{t}", tag=f"sum{t}")
-            cols = slice(t * P, (t + 1) * P)
-            width = half if t == 0 else S
-            for j0 in range(0, S, width):
+            width = HALF if t == 0 else S
+            for u in range(S // width):
+                tag = "spare" if (t, u) == (0, 0) else f"sum{t}"
+                y_bank = psum.tile([P, S], F32, name=f"y_bank{t}_{u}", tag=tag)
                 nc.tensor.matmul_mx(
-                    out=y_bank[:, j0 : j0 + width],
-                    lhsT=w1_codes[:, cols].bitcast(FP8X4),
-                    lhsT_scale=w1_scales[:, cols],
-                    rhs=picked_words[:, j0 : j0 + width].bitcast(FP8X4),
-                    rhs_scale=picked_scales[:, j0 : j0 + width],
+                    out=y_bank[:, :width],
+                    lhsT=w1_codes[:, span(t, P)].bitcast(FP8X4),
+                    lhsT_scale=w1_scales[:, span(t, P)],
+                    rhs=picked_words[:, span(u, width)].bitcast(FP8X4),
+                    rhs_scale=picked_scales[:, span(u, width)],
                     start=True,
                     stop=True,
                 )
-            nc.scalar.activation(
-                out=windows[t][:, :S], in_=y_bank[:], func=ACT.Copy, accum_out=sums[:, t : t + 1]
-            )
+                nc.scalar.activation(
+                    out=windows[t][:, span(u, width)],
+                    in_=y_bank[:, :width],
+                    func=ACT.Copy,
+                    accum_out=row_sums[:, span(PACK + u if t == 0 else t, 1)],
+                )
+            if t > 0:
+                y_copies[t] = keep.tile([P, S], F32, name=f"y_copy{t}")
+                nc.sync.dma_start(y_copies[t][:], windows[t][:, :S])
+        nc.scalar.activation(
+            out=row_sums[:, 0:1], in_=row_sums[:, span(PACK, 1)], func=ACT.Identity, bias=row_sums[:, PACK + 1 :]
+        )
 
         wgt_bank = psum.tile([P, S], F32, name="wgt_bank", tag="spare")
         nc.tensor.transpose(wgt_bank[:, :P], wgt_rows, ident[:])
@@ -131,147 +147,126 @@ def tile_picked_ymoran_geary_p_kernel(
         nc.scalar.copy(wgt_cols[:], wgt_bank[:, : D * BLOCKS])
 
         neg_mean = keep.tile([P, PACK], F32, name="neg_mean")
-        nc.scalar.activation(out=neg_mean[:], in_=sums[:], func=ACT.Copy, scale=-1.0 / S)
-        squares = keep.tile([P, PACK], F32, name="squares")
+        nc.scalar.activation(out=neg_mean[:], in_=row_sums[:, :PACK], func=ACT.Copy, scale=-1.0 / S)
+        dev2_sums = keep.tile([P, PACK], F32, name="dev2_sums")
         dev2 = keep.tile([P, S], F32, name="dev2")
 
         sum_banks = [psum.tile([P, S], F32, name=f"sum_bank{b}", tag=f"sum{b}") for b in range(BLOCKS)]
-        units = PACK * D
         squared = {}
         gathered = {}
-        weighted = {}
 
-        def differences(n):
+        def add_transposed(bank_cols, source, start, stop):
+            nc.tensor.matmul(bank_cols, source, ident[:], is_transpose=True, start=start, stop=stop)
+
+        def square_differences(n):
             t, d = divmod(n, D)
-            diff_bank = psum.tile([P, S], F32, name=f"diff_bank{n}", tag=f"diff{n % 3}")
-            for b in range(BLOCKS):
-                nc.tensor.matmul(
-                    diff_bank[:, b * P : (b + 1) * P],
-                    windows[t][:, b * P : (b + 1) * P],
-                    ident[:],
-                    is_transpose=True,
-                    start=(b == 0),
-                    stop=False,
-                )
             if n == 0:
-                gathered[0] = keep.tile([P, D + 1, S], F32, name="negated0")
+                gathered[0] = keep.tile([P, D + 1, S], F32, name="gathered0")
             elif d == 1 and t >= 1:
-                gathered[t] = keep.tile([P, D, S], F32, name=f"negated{t}", tag=f"squared{n - D}")
-            negated = gathered[0][:, n, :] if n <= D else gathered[(n - 1) // D][:, (n - 1) % D, :]
-            nc.vector.tensor_scalar(
-                negated, windows[t][:].indirect(lists[d][:]), -1.0, 0.0, ALU.mult, ALU.add
-            )
-            for b in range(BLOCKS):
-                nc.tensor.matmul(
-                    diff_bank[:, b * P : (b + 1) * P],
-                    negated[:, b * P : (b + 1) * P],
-                    ident[:],
-                    is_transpose=True,
-                    start=False,
-                    stop=(b == BLOCKS - 1),
-                )
+                gathered[t] = keep.tile([P, D, S], F32, name=f"gathered{t}", tag=f"squared{n - D}")
+            looked_up = gathered[0][:, n, :] if n <= D else gathered[(n - 1) // D][:, (n - 1) % D, :]
             squared[n] = keep.tile([P, S], F32, name=f"squared{n}", tag=f"squared{n}")
-            width = half if n == units - 1 else S
-            for j0 in range(0, S, width):
-                nc.scalar.activation(
-                    out=squared[n][:, j0 : j0 + width], in_=diff_bank[:, j0 : j0 + width], func=ACT.Square
-                )
+            width = HALF if n == STEPS - 1 else S
+            for u in range(S // width):
+                cols = span(u, width)
+                blocks = range(u * width // P, (u + 1) * width // P)
+                tag = "spare" if u else f"diff{n % DIFF_BANKS}"
+                diff_bank = psum.tile([P, S], F32, name=f"diff_bank{n}_{u}", tag=tag)
+                neighbours = windows[t][:].indirect(lists[d][:, span(u, width // STRIPE)])
+                if t == 0:
+                    for b in blocks:
+                        add_transposed(diff_bank[:, span(b, P)], windows[t][:, span(b, P)], b == 0, False)
+                    nc.vector.tensor_scalar(looked_up[:, cols], neighbours, -1.0, 0.0, ALU.mult, ALU.add)
+                else:
+                    nc.vector.tensor_tensor(looked_up[:, cols], neighbours, y_copies[t][:, cols], ALU.subtract)
+                for b in blocks:
+                    add_transposed(
+                        diff_bank[:, span(b, P)], looked_up[:, span(b, P)], t > 0, t > 0 or b == BLOCKS - 1
+                    )
+                nc.scalar.activation(out=squared[n][:, cols], in_=diff_bank[:, cols], func=ACT.Square)
 
         def weigh_and_add(n):
             t, d = divmod(n, D)
-            weighted[n] = keep.tile([P, S], F32, name=f"weighted{n}")
+            weighted = keep.tile([P, S], F32, name=f"weighted{n}")
             for b in range(BLOCKS):
-                cols = slice(b * P, (b + 1) * P)
-                w_col = wgt_cols[:, BLOCKS * d + b : BLOCKS * d + b + 1]
-                if d == 1:
-                    nc.vector.scalar_tensor_tensor(
-                        weighted[n][:, cols], squared[n][:, cols], w_col, weighted[n - 1][:, cols], ALU.mult, ALU.add
-                    )
-                elif n == units - 1:
-                    nc.vector.tensor_scalar(weighted[n][:, cols], squared[n][:, cols], w_col, None, ALU.mult)
+                cols = span(b, P)
+                wgt_col = wgt_cols[:, span(BLOCKS * d + b, 1)]
+                if d == 1 or t == PACK - 1:
+                    nc.vector.tensor_scalar(weighted[:, cols], squared[n][:, cols], wgt_col, None, ALU.mult)
                 else:
                     nc.scalar.activation(
-                        out=weighted[n][:, cols], in_=squared[n][:, cols], func=ACT.Copy, scale=w_col
+                        out=weighted[:, cols], in_=squared[n][:, cols], func=ACT.Copy, scale=wgt_col
                     )
-            if d == 0:
-                return
             for b in range(BLOCKS):
-                nc.tensor.matmul(
-                    sum_banks[b][:, t * P : (t + 1) * P],
-                    weighted[n][:, b * P : (b + 1) * P],
-                    ident[:],
-                    is_transpose=True,
-                    start=(n == 1),
-                    stop=(n == units - 1),
-                )
+                add_transposed(sum_banks[b][:, span(t, P)], weighted[:, span(b, P)], n == 0, n == STEPS - 1)
 
-        def sum_of_squares(t):
+        def sum_dev2(t):
             nc.scalar.activation(
                 out=dev2[:],
                 in_=windows[t][:, :S],
                 func=ACT.Square,
-                bias=neg_mean[:, t : t + 1],
-                accum_out=squares[:, t : t + 1],
+                bias=neg_mean[:, span(t, 1)],
+                accum_out=dev2_sums[:, span(t, 1)],
             )
 
         for t in range(PACK):
             n = D * t
-            differences(n)
+            square_differences(n)
             if t == 0:
-                sum_of_squares(t)
+                sum_dev2(t)
             else:
                 weigh_and_add(n - 1)
+            square_differences(n + 1)
             weigh_and_add(n)
-            differences(n + 1)
             if t > 0:
-                sum_of_squares(t)
+                sum_dev2(t)
             weigh_and_add(n + 1)
-            differences(n + 2)
-        weigh_and_add(units - 1)
+            square_differences(n + 2)
+        weigh_and_add(STEPS - 1)
+
         var = keep.tile([P, PACK], F32, name="var")
-        nc.vector.tensor_scalar(var[:], squares[:], 1.0 / S, EPS, ALU.mult, ALU.add)
+        nc.vector.tensor_scalar(var[:], dev2_sums[:], 1.0 / S, VAR_FLOOR, ALU.mult, ALU.add)
         inv_var = keep.tile([P, PACK], F32, name="inv_var")
         nc.vector.reciprocal(inv_var[:], var[:])
         factor = keep.tile([P, PACK], F32, name="factor")
         nc.vector.tensor_tensor(factor[:], inv_var[:], unit_sb, ALU.mult)
 
-        out_view = out.rearrange("(h p) j -> p h j", p=P)
-        zz_tiles = [keep.tile([P, P, PACK], BF16, name=f"zz{b}", align_bytes=64) for b in range(BLOCKS)]
+        zz = [keep.tile([P, P, PACK], BF16, name=f"zz{b}", align_bytes=64) for b in range(BLOCKS)]
         for t in range(PACK):
             nc.scalar.activation(
-                out=zz_tiles[BLOCKS - 1][:, :, t],
-                in_=sum_banks[BLOCKS - 1][:, t * P : (t + 1) * P],
-                func=ACT.Copy,
-                scale=factor[:, t : t + 1],
+                out=zz[0][:, :, t], in_=sum_banks[0][:, span(t, P)], func=ACT.Copy, scale=factor[:, span(t, 1)]
             )
-        for b in range(BLOCKS):
-            zz = zz_tiles[b]
-            if b < BLOCKS - 1:
-                nc.vector.tensor_tensor(
-                    zz[:],
-                    sum_banks[b][:].rearrange("p (t j) -> p j t", t=PACK),
-                    factor[:].unsqueeze(1).to_broadcast([P, P, PACK]),
-                    ALU.mult,
-                )
+        for b in range(1, BLOCKS):
+            nc.vector.tensor_tensor(
+                zz[b][:],
+                sum_banks[b][:].rearrange("p (t j) -> p j t", t=PACK),
+                factor[:].unsqueeze(1).to_broadcast([P, P, PACK]),
+                ALU.mult,
+            )
+
+        out_view = out.rearrange("(h p) j -> p h j", p=P)
+        for b in (1, 2, 0, 3):
             zz_codes = keep.tile([P, P], U32, name=f"zz_codes{b}", align_bytes=64)
             zz_scales = keep.tile([P, P], U8, name=f"zz_scales{b}", align_bytes=64)
             nc.vector.quantize_mx(
                 out=zz_codes[:].bitcast(FP8X4),
                 scales=zz_scales[:],
-                in_=zz[:].rearrange("p j t -> p (j t)"),
+                in_=zz[b][:].rearrange("p j t -> p (j t)"),
             )
-            out_bank = psum.tile([P, S], F32, name=f"out_bank{b}", tag=f"diff{b}" if b < 3 else "spare")
+            out_bank = psum.tile([P, S], F32, name=f"out_bank{b}", tag=f"diff{b}" if b < DIFF_BANKS else "spare")
             for h in range(N // P):
-                cols = slice(h * P, (h + 1) * P)
                 nc.tensor.matmul_mx(
-                    out=out_bank[:, cols],
-                    lhsT=wo_codes[:, cols].bitcast(FP8X4),
-                    lhsT_scale=wo_scales[:, cols],
+                    out=out_bank[:, span(h, P)],
+                    lhsT=wo_codes[:, span(h, P)].bitcast(FP8X4),
+                    lhsT_scale=wo_scales[:, span(h, P)],
                     rhs=zz_codes[:].bitcast(FP8X4),
                     rhs_scale=zz_scales[:],
                     start=True,
                     stop=True,
                 )
             result = keep.tile([P, N // P, P], F32, name=f"result{b}")
-            nc.scalar.copy(result[:].rearrange("p h j -> p (h j)"), out_bank[:, :N])
-            nc.sync.dma_start(out_view[:, :, b * P : (b + 1) * P], result[:])
+            if b == BLOCKS - 1:
+                nc.vector.tensor_copy(result[:].rearrange("p h j -> p (h j)"), out_bank[:, :N])
+            else:
+                nc.scalar.copy(result[:].rearrange("p h j -> p (h j)"), out_bank[:, :N])
+            nc.sync.dma_start(out_view[:, :, span(b, P)], result[:])

from contextlib import ExitStack

import concourse.mybir as mybir
from concourse.masks import make_identity

K, H, T, S, N, D = 512, 512, 2048, 512, 256, 3
P = 128
PACK = 4
QUADRANT = 32
STRIPE = 16
BLOCKS = S // P
HALF = S // 2
STEPS = PACK * D
VAR_FLOOR = 0.05
WINDOW = 2048
DIFF_BANKS = 3
W1_VECTOR_SHARE = 80
FLOPS = 2 * K * H * S + 2 * H * N * S

F32 = mybir.dt.float32
BF16 = mybir.dt.bfloat16
I32 = mybir.dt.int32
U32 = mybir.dt.uint32
U16 = mybir.dt.uint16
U8 = mybir.dt.uint8
FP8X4 = mybir.dt.float8_e4m3fn_x4
ALU = mybir.AluOpType
ACT = mybir.ActivationFunctionType


def span(index, width):
    return slice(index * width, (index + 1) * width)


def tile_picked_ymoran_geary_p_kernel(
    tc, x_words, x_scales, w1, wgt, unit, wo, offs, pos1, pos2, pos3, out
):
    nc = tc.nc
    with ExitStack() as ctx:
        keep = ctx.enter_context(tc.tile_pool(name="keep", bufs=1))
        psum = ctx.enter_context(tc.psum_pool(name="psum", bufs=1))

        table_scales = keep.tile([P, T], U8, name="table_scales", tag="scales_then_rows")
        nc.vector.memset(table_scales[:, : T // 2].bitcast(I32), 0)
        nc.gpsimd.memset(table_scales[:, T // 2 :].bitcast(I32), 0)
        offs_sb = keep.tile([P, S // STRIPE], U16, name="offs_sb")
        nc.sync.dma_start(offs_sb[:], offs)
        lists = [keep.tile([P, S // STRIPE], U16, name=f"pos_sb{d}") for d in range(D)]
        nc.sync.dma_start(lists[0][:], pos1)
        nc.sync.dma_start(lists[1][:], pos2)
        w1_raw = keep.tile([P, PACK, H], F32, name="w1_raw")
        nc.sync.dma_start(w1_raw[:], w1.rearrange("(p j) c -> p j c", j=PACK))
        for q in range(P // QUADRANT):
            nc.sync.dma_start(
                table_scales[QUADRANT * q : QUADRANT * q + 4, :].bitcast(I32),
                x_scales[0, span(q, 4), :].bitcast(I32),
            )
        table_words = keep.tile([P, T], I32, name="table_words")
        nc.sync.dma_start(table_words[:], x_words[0].rearrange("p n t -> p (n t)").bitcast(I32))
        wo_raw = keep.tile([P, PACK, N], F32, name="wo_raw")
        nc.sync.dma_start(wo_raw[:], wo.rearrange("(p j) m -> p j m", j=PACK))
        nc.sync.dma_start(lists[2][:], pos3)
        ident = keep.tile([P, P], F32, name="ident")
        make_identity(nc, ident[:])

        windows = [keep.tile([P, WINDOW], F32, name=f"window{t}") for t in range(PACK)]

        picked_scales = keep.tile([P, S], U8, name="picked_scales", align_bytes=64)
        nc.vector.tensor_copy(picked_scales[:], table_scales[:].indirect(offs_sb[:]))

        rows = keep.tile([P, P + PACK], F32, name="rows", tag="scales_then_rows")
        nc.vector.memset(rows[:], 0.0)
        wgt_rows = rows[:, :P]
        unit_sb = rows[:, P:]
        piece_step = P + 1
        nc.sync.dma_start(
            rows[: D * BLOCKS, :P],
            wgt.rearrange("d r (b j) -> (d r b) j", j=P)[0 : (D * BLOCKS - 1) * piece_step + 1 : piece_step, :],
        )
        nc.sync.dma_start(unit_sb, unit.rearrange("(p t) o -> p (t o)", t=PACK))

        w1_bf = keep.tile([P, PACK, P, PACK], BF16, name="w1_bf", align_bytes=64)
        w1_dst = w1_bf[:].rearrange("p t m j -> p m j t")
        w1_src = w1_raw[:].rearrange("p j (m t) -> p m j t", t=PACK)
        nc.vector.tensor_copy(w1_dst[:, :W1_VECTOR_SHARE], w1_src[:, :W1_VECTOR_SHARE])
        nc.scalar.copy(w1_dst[:, W1_VECTOR_SHARE:], w1_src[:, W1_VECTOR_SHARE:])
        w1_codes = keep.tile([P, H], U32, name="w1_codes", align_bytes=64)
        w1_scales = keep.tile([P, H], U8, name="w1_scales", align_bytes=64)
        nc.vector.quantize_mx(
            out=w1_codes[:].bitcast(FP8X4),
            scales=w1_scales[:],
            in_=w1_bf[:].rearrange("p t m j -> p (t m j)"),
        )

        picked_words = keep.tile([P, S], I32, name="picked_words", align_bytes=64)
        for u in range(S // HALF):
            nc.vector.tensor_copy(
                picked_words[:, span(u, HALF)].bitcast(U32),
                table_words[:].bitcast(U32).indirect(offs_sb[:, span(u, HALF // STRIPE)]),
            )

        wo_bf = keep.tile([P, N, PACK], BF16, name="wo_bf", align_bytes=64)
        nc.vector.tensor_copy(
            wo_bf[:].rearrange("p (c i) j -> p c j i", i=4),
            wo_raw[:].rearrange("p j (c i) -> p c j i", i=4),
        )
        wo_codes = keep.tile([P, N], U32, name="wo_codes", align_bytes=64)
        wo_scales = keep.tile([P, N], U8, name="wo_scales", align_bytes=64)
        nc.vector.quantize_mx(
            out=wo_codes[:].bitcast(FP8X4),
            scales=wo_scales[:],
            in_=wo_bf[:].rearrange("p m j -> p (m j)"),
        )

        row_sums = keep.tile([P, PACK + 2], F32, name="row_sums")
        y_copies = {}
        for t in range(PACK):
            width = HALF if t == 0 else S
            for u in range(S // width):
                tag = "spare" if (t, u) == (0, 0) else f"sum{t}"
                y_bank = psum.tile([P, S], F32, name=f"y_bank{t}_{u}", tag=tag)
                nc.tensor.matmul_mx(
                    out=y_bank[:, :width],
                    lhsT=w1_codes[:, span(t, P)].bitcast(FP8X4),
                    lhsT_scale=w1_scales[:, span(t, P)],
                    rhs=picked_words[:, span(u, width)].bitcast(FP8X4),
                    rhs_scale=picked_scales[:, span(u, width)],
                    start=True,
                    stop=True,
                )
                nc.scalar.activation(
                    out=windows[t][:, span(u, width)],
                    in_=y_bank[:, :width],
                    func=ACT.Copy,
                    accum_out=row_sums[:, span(PACK + u if t == 0 else t, 1)],
                )
            if t > 0:
                y_copies[t] = keep.tile([P, S], F32, name=f"y_copy{t}")
                nc.sync.dma_start(y_copies[t][:], windows[t][:, :S])
        nc.scalar.activation(
            out=row_sums[:, 0:1], in_=row_sums[:, span(PACK, 1)], func=ACT.Identity, bias=row_sums[:, PACK + 1 :]
        )

        wgt_bank = psum.tile([P, S], F32, name="wgt_bank", tag="spare")
        nc.tensor.transpose(wgt_bank[:, :P], wgt_rows, ident[:])
        wgt_cols = keep.tile([P, D * BLOCKS], F32, name="wgt_cols")
        nc.scalar.copy(wgt_cols[:], wgt_bank[:, : D * BLOCKS])

        neg_mean = keep.tile([P, PACK], F32, name="neg_mean")
        nc.scalar.activation(out=neg_mean[:], in_=row_sums[:, :PACK], func=ACT.Copy, scale=-1.0 / S)
        dev2_sums = keep.tile([P, PACK], F32, name="dev2_sums")
        dev2 = keep.tile([P, S], F32, name="dev2")

        sum_banks = [psum.tile([P, S], F32, name=f"sum_bank{b}", tag=f"sum{b}") for b in range(BLOCKS)]
        squared = {}
        gathered = {}

        def add_transposed(bank_cols, source, start, stop):
            nc.tensor.matmul(bank_cols, source, ident[:], is_transpose=True, start=start, stop=stop)

        def square_differences(n):
            t, d = divmod(n, D)
            if n == 0:
                gathered[0] = keep.tile([P, D + 1, S], F32, name="gathered0")
            elif d == 1 and t >= 1:
                gathered[t] = keep.tile([P, D, S], F32, name=f"gathered{t}", tag=f"squared{n - D}")
            looked_up = gathered[0][:, n, :] if n <= D else gathered[(n - 1) // D][:, (n - 1) % D, :]
            squared[n] = keep.tile([P, S], F32, name=f"squared{n}", tag=f"squared{n}")
            width = HALF if n == STEPS - 1 else S
            for u in range(S // width):
                cols = span(u, width)
                blocks = range(u * width // P, (u + 1) * width // P)
                tag = "spare" if u else f"diff{n % DIFF_BANKS}"
                diff_bank = psum.tile([P, S], F32, name=f"diff_bank{n}_{u}", tag=tag)
                neighbours = windows[t][:].indirect(lists[d][:, span(u, width // STRIPE)])
                if t == 0:
                    for b in blocks:
                        add_transposed(diff_bank[:, span(b, P)], windows[t][:, span(b, P)], b == 0, False)
                    nc.vector.tensor_scalar(looked_up[:, cols], neighbours, -1.0, 0.0, ALU.mult, ALU.add)
                else:
                    nc.vector.tensor_tensor(looked_up[:, cols], neighbours, y_copies[t][:, cols], ALU.subtract)
                for b in blocks:
                    add_transposed(
                        diff_bank[:, span(b, P)], looked_up[:, span(b, P)], t > 0, t > 0 or b == BLOCKS - 1
                    )
                nc.scalar.activation(out=squared[n][:, cols], in_=diff_bank[:, cols], func=ACT.Square)

        def weigh_and_add(n):
            t, d = divmod(n, D)
            weighted = keep.tile([P, S], F32, name=f"weighted{n}")
            for b in range(BLOCKS):
                cols = span(b, P)
                wgt_col = wgt_cols[:, span(BLOCKS * d + b, 1)]
                if d == 1 or t == PACK - 1:
                    nc.vector.tensor_scalar(weighted[:, cols], squared[n][:, cols], wgt_col, None, ALU.mult)
                else:
                    nc.scalar.activation(
                        out=weighted[:, cols], in_=squared[n][:, cols], func=ACT.Copy, scale=wgt_col
                    )
            for b in range(BLOCKS):
                add_transposed(sum_banks[b][:, span(t, P)], weighted[:, span(b, P)], n == 0, n == STEPS - 1)

        def sum_dev2(t):
            nc.scalar.activation(
                out=dev2[:],
                in_=windows[t][:, :S],
                func=ACT.Square,
                bias=neg_mean[:, span(t, 1)],
                accum_out=dev2_sums[:, span(t, 1)],
            )

        for t in range(PACK):
            n = D * t
            square_differences(n)
            if t == 0:
                sum_dev2(t)
            else:
                weigh_and_add(n - 1)
            square_differences(n + 1)
            weigh_and_add(n)
            if t > 0:
                sum_dev2(t)
            weigh_and_add(n + 1)
            square_differences(n + 2)
        weigh_and_add(STEPS - 1)

        var = keep.tile([P, PACK], F32, name="var")
        nc.vector.tensor_scalar(var[:], dev2_sums[:], 1.0 / S, VAR_FLOOR, ALU.mult, ALU.add)
        inv_var = keep.tile([P, PACK], F32, name="inv_var")
        nc.vector.reciprocal(inv_var[:], var[:])
        factor = keep.tile([P, PACK], F32, name="factor")
        nc.vector.tensor_tensor(factor[:], inv_var[:], unit_sb, ALU.mult)

        zz = [keep.tile([P, P, PACK], BF16, name=f"zz{b}", align_bytes=64) for b in range(BLOCKS)]
        for t in range(PACK):
            nc.scalar.activation(
                out=zz[0][:, :, t], in_=sum_banks[0][:, span(t, P)], func=ACT.Copy, scale=factor[:, span(t, 1)]
            )
        for b in range(1, BLOCKS):
            nc.vector.tensor_tensor(
                zz[b][:],
                sum_banks[b][:].rearrange("p (t j) -> p j t", t=PACK),
                factor[:].unsqueeze(1).to_broadcast([P, P, PACK]),
                ALU.mult,
            )

        out_view = out.rearrange("(h p) j -> p h j", p=P)
        for b in (1, 2, 0, 3):
            zz_codes = keep.tile([P, P], U32, name=f"zz_codes{b}", align_bytes=64)
            zz_scales = keep.tile([P, P], U8, name=f"zz_scales{b}", align_bytes=64)
            nc.vector.quantize_mx(
                out=zz_codes[:].bitcast(FP8X4),
                scales=zz_scales[:],
                in_=zz[b][:].rearrange("p j t -> p (j t)"),
            )
            out_bank = psum.tile([P, S], F32, name=f"out_bank{b}", tag=f"diff{b}" if b < DIFF_BANKS else "spare")
            for h in range(N // P):
                nc.tensor.matmul_mx(
                    out=out_bank[:, span(h, P)],
                    lhsT=wo_codes[:, span(h, P)].bitcast(FP8X4),
                    lhsT_scale=wo_scales[:, span(h, P)],
                    rhs=zz_codes[:].bitcast(FP8X4),
                    rhs_scale=zz_scales[:],
                    start=True,
                    stop=True,
                )
            result = keep.tile([P, N // P, P], F32, name=f"result{b}")
            if b == BLOCKS - 1:
                nc.vector.tensor_copy(result[:].rearrange("p h j -> p (h j)"), out_bank[:, :N])
            else:
                nc.scalar.copy(result[:].rearrange("p h j -> p (h j)"), out_bank[:, :N])
            nc.sync.dma_start(out_view[:, :, span(b, P)], result[:])
